import numpy as np
import ml_dtypes


def mxq(x, axis, fmt="e4m3"):
    dtype, down = {"e4m3": (ml_dtypes.float8_e4m3fn, 7), "e5m2": (ml_dtypes.float8_e5m2, 14)}[fmt]
    v = np.moveaxis(np.asarray(x, np.float32).astype(ml_dtypes.bfloat16).astype(np.float64), axis, -1)
    blocks = v.reshape(v.shape[:-1] + (-1, 32))
    amax = np.abs(blocks).max(-1, keepdims=True)
    byte = np.maximum(np.where(amax > 0, np.frexp(amax)[1] - 1 + 127, 0) - down, 1)
    scale = np.exp2(byte - 127.0)
    codes = (blocks / scale).astype(np.float32).astype(dtype).astype(np.float64)
    return np.moveaxis((codes * scale).reshape(v.shape), -1, axis)


WIDE = False


def mx_kscale(k):
    if not WIDE:
        return np.ones(k)
    levels = np.array([10, -10, 5, -5, 0])
    if k % 512:
        return np.exp2(np.random.permutation(np.resize(levels, k // 32))).repeat(32)
    a = np.empty((k // 512, 16))
    for p in range(k // 512):
        a[p, :8] = np.random.permutation(np.resize(levels, 8))
        for g in range(8):
            far = levels[np.abs(levels - a[p, g]) >= 10]
            a[p, g + 8] = far[np.random.randint(len(far))]
    return np.exp2(a.ravel()).repeat(32)


BF16 = ml_dtypes.bfloat16


def bf(x):
    return np.asarray(x, np.float32).astype(BF16)


def f64(x):
    return np.asarray(x).astype(np.float64)


L, T, N, K, M = 4, 512, 512, 512, 1024


def pam4_points():
    return np.array([-3.0, -1.0, 1.0, 3.0]) / np.sqrt(5.0)


def softmax_last(e):
    w = np.exp(e - e.max(axis=-1, keepdims=True))
    return w / w.sum(axis=-1, keepdims=True)


def pam4_posterior_mean(s, nv):
    p = pam4_points()
    d = s[:, :, None] - p[None, None, :]
    e = -(d * d) / (2.0 * nv[None, :, None])
    pi = softmax_last(e)
    return np.sum(p[None, None, :] * pi, axis=-1)


def draw0():
    c, t = mx_kscale(N), mx_kscale(K)
    return {
        "y": bf(np.random.standard_normal((L, T, N)) * c),
        "v": bf(np.random.standard_normal((L, N, K)) / np.sqrt(N) / c[:, None]),
        "a": bf(np.random.standard_normal((L, K)) / np.sqrt(L)),
        "nv": bf(np.random.uniform(0.1, 0.4, (K,))),
        "g": bf((1.0 + 0.1 * np.random.standard_normal(K)) * t),
        "h0": bf(np.random.standard_normal((K, M)) / np.sqrt(K) / t[:, None]),
        "y0": bf(np.random.standard_normal((T, M))),
    }


def core(y, v, a, nv, g, h0, y0):
    z = mxq(f64(y), 2, "e4m3") @ mxq(f64(v), 1, "e4m3")
    s = np.sum(f64(a)[:, None, :] * z, axis=0)
    xh = pam4_posterior_mean(s, f64(nv))
    u = f64(g)[None, :] * xh
    return f64(y0) - (mxq(u, 1, "e4m3") @ mxq(f64(h0), 0, "e4m3"))


def e4m3fn_bytes(y):
    return np.clip(np.asarray(y, np.float64), -448.0, 448.0).astype(np.float32).astype(ml_dtypes.float8_e4m3fn).view(np.uint8)


def e4m3fn_values(b):
    return np.asarray(b, np.uint8).view(ml_dtypes.float8_e4m3fn).astype(np.float64)


def setup_inputs():
    d = draw0()
    x0 = np.asarray(d['y']).astype(np.float64)
    s = (np.max(np.abs(x0), axis=(0, 1), keepdims=True) / 448.0).astype(np.float32)
    out = {}
    for k, v in d.items():
        if k == 'y':
            out['y_bytes'] = e4m3fn_bytes(x0 / s.astype(np.float64))
            out['y_scale'] = s
        else:
            out[k] = v
    return out


def reference(y_bytes, y_scale, v, a, nv, g, h0, y0):
    return core(e4m3fn_values(y_bytes) * y_scale.astype(np.float64), v, a, nv, g, h0, y0)

@@ -1,0 +1,317 @@
+import math
+from contextlib import ExitStack
+
+import concourse.mybir as mybir
+from concourse.masks import make_identity
+
+L, T, N, K, M = 4, 512, 512, 512, 1024
+FLOPS = 2 * (L * T * N * K + T * K * M)
+
+F32 = mybir.dt.float32
+BF16 = mybir.dt.bfloat16
+U32 = mybir.dt.uint32
+U8 = mybir.dt.uint8
+FP8 = mybir.dt.float8_e4m3fn
+FP8X4 = mybir.dt.float8_e4m3fn_x4
+ALU = mybir.AluOpType
+ACT = mybir.ActivationFunctionType
+
+P = 128
+PACK = 4
+BANK = 512
+C = 1.0 / math.sqrt(5.0)
+EXP_CAP = 40.0
+TINY = 2.0 ** -60
+
+
+def tile_cellfreelsfdpaminterferenceresidual_kernel(tc, y_bytes, y_scale, v, a, nv, g, h0, y0, out):
+    nc = tc.nc
+    with ExitStack() as ctx:
+        sb = ctx.enter_context(tc.tile_pool(name="sb", bufs=1))
+        ps = ctx.enter_context(tc.psum_pool(name="ps", bufs=1))
+        ctx.enter_context(tc.manual_schedule())
+
+        def sbt(name, shape, dtype):
+            return sb.tile(shape, dtype, name=name, align_bytes=64)
+
+        scale_col = sbt("scale_col", [P, PACK], F32)
+        nc.sync.dma_start(out=scale_col[:], in_=y_scale.rearrange("a b (p t) -> p (a b t)", t=PACK))
+        nv_sb = sbt("nv_sb", [P, PACK], BF16)
+        a_sb = sbt("a_sb", [P, L, PACK], BF16)
+        g_sb = sbt("g_sb", [P, PACK], BF16)
+        nc.scalar.dma_start(out=nv_sb[:], in_=nv.rearrange("(p t) -> p t", t=PACK))
+        nc.scalar.dma_start(out=a_sb[:], in_=a.rearrange("l (p t) -> p l t", t=PACK))
+        nc.scalar.dma_start(out=g_sb[:], in_=g.rearrange("(p t) -> p t", t=PACK))
+        y_codes8 = []
+        v_raw = []
+        for l in range(L):
+            y_codes8.append(sbt("y_fp8_%d" % l, [P, PACK * N], U8))
+            v_raw.append(sbt("v_raw_%d" % l, [P, PACK, K], BF16))
+            nc.sync.dma_start(out=y_codes8[l][:], in_=y_bytes[l].rearrange("(p j) n -> p (j n)", j=PACK))
+            nc.sync.dma_start(out=v_raw[l][:], in_=v[l].rearrange("(p j) k -> p j k", j=PACK))
+        h_raw = sbt("h_raw", [P, PACK, M], BF16)
+        nc.sync.dma_start(out=h_raw[:], in_=h0.rearrange("(p j) m -> p j m", j=PACK))
+        y0_sb = sbt("y0_sb", [P, PACK, M], BF16)
+        nc.sync.dma_start(out=y0_sb[:], in_=y0.rearrange("(p j) m -> p j m", j=PACK))
+
+        ident = sbt("ident", [P, P], F32)
+        make_identity(nc, ident[:])
+
+        def par(name):
+            return sbt(name, [P, PACK], F32)
+
+        inv_nv = par("inv_nv")
+        nc.vector.reciprocal(out=inv_nv[:], in_=nv_sb[:])
+        ratio = par("ratio")
+        nc.scalar.activation(out=ratio[:], in_=inv_nv[:], func=ACT.Exp, scale=-0.8)
+        c_over_nv = par("c_over_nv")
+        nc.gpsimd.tensor_scalar(out=c_over_nv[:], in0=inv_nv[:], scalar1=C, scalar2=0.0, op0=ALU.mult, op1=ALU.add)
+        weight = sbt("weight", [P, L, PACK], F32)
+        nc.gpsimd.tensor_tensor(out=weight[:], in0=a_sb[:], in1=c_over_nv[:].unsqueeze(1).to_broadcast([P, L, PACK]), op=ALU.mult)
+        log_ratio = par("log_ratio")
+        nc.gpsimd.tensor_scalar(out=log_ratio[:], in0=inv_nv[:], scalar1=-0.8, scalar2=0.0, op0=ALU.mult, op1=ALU.add)
+        x_hi = par("x_hi")
+        nc.gpsimd.tensor_scalar(out=x_hi[:], in0=inv_nv[:], scalar1=0.4, scalar2=EXP_CAP / 2, op0=ALU.mult, op1=ALU.add)
+        x_lo = par("x_lo")
+        nc.gpsimd.tensor_scalar(out=x_lo[:], in0=inv_nv[:], scalar1=-0.4, scalar2=-EXP_CAP / 2, op0=ALU.mult, op1=ALU.add)
+        one_minus_ratio = par("one_minus_ratio")
+        nc.gpsimd.tensor_scalar(out=one_minus_ratio[:], in0=ratio[:], scalar1=-1.0, scalar2=1.0, op0=ALU.mult, op1=ALU.add)
+        k1_unit = par("k1_unit")
+        nc.gpsimd.tensor_scalar(out=k1_unit[:], in0=ratio[:], scalar1=6.0 * C, scalar2=-2.0 * C, op0=ALU.mult, op1=ALU.add)
+        k1 = par("k1")
+        nc.gpsimd.tensor_tensor(out=k1[:], in0=k1_unit[:], in1=g_sb[:], op=ALU.mult)
+        half_sign = par("half_sign")
+        nc.gpsimd.tensor_scalar(out=half_sign[:], in0=k1[:], scalar1=0.0, scalar2=0.5, op0=ALU.is_ge, op1=ALU.subtract)
+        k1_sign = par("k1_sign")
+        nc.gpsimd.tensor_scalar(out=k1_sign[:], in0=half_sign[:], scalar1=2.0, scalar2=0.0, op0=ALU.mult, op1=ALU.add)
+        k1_abs = par("k1_abs")
+        nc.gpsimd.tensor_tensor(out=k1_abs[:], in0=k1[:], in1=k1_sign[:], op=ALU.mult)
+        k1_floor = par("k1_floor")
+        nc.gpsimd.tensor_scalar(out=k1_floor[:], in0=k1_abs[:], scalar1=1.0, scalar2=TINY, op0=ALU.mult, op1=ALU.max)
+        g_signed = par("g_signed")
+        nc.gpsimd.tensor_tensor(out=g_signed[:], in0=k1_sign[:], in1=g_sb[:], op=ALU.mult)
+        k2_signed = par("k2_signed")
+        nc.gpsimd.tensor_scalar(out=k2_signed[:], in0=g_signed[:], scalar1=3.0 * C, scalar2=0.0, op0=ALU.mult, op1=ALU.add)
+        inv_k1 = par("inv_k1")
+
+        scale_bank = ps.tile([P, BANK], F32, name="scale_bank")
+        for t in range(PACK):
+            nc.tensor.transpose(scale_bank[:, t:BANK:PACK], scale_col[:, t:t + 1].to_broadcast([P, P]), ident[:])
+
+        y_val = {}
+        turn_bank = {}
+        y_turned = [sbt("y_turned_%d" % l, [P, T * PACK], BF16) for l in range(L)]
+        v_grouped = [sbt("v_grouped_%d" % l, [P, K * PACK], BF16) for l in range(L)]
+        y_q = [sbt("y_q_%d" % l, [P, T], U32) for l in range(L)]
+        y_s = [sbt("y_s_%d" % l, [P, T], U8) for l in range(L)]
+        v_q = [sbt("v_q_%d" % l, [P, K], U32) for l in range(L)]
+        v_s = [sbt("v_s_%d" % l, [P, K], U8) for l in range(L)]
+        z_bank = {}
+        x = [sbt("x_%d" % t, [P, T], F32) for t in range(PACK)]
+        x_cl = [sbt("x_cl_%d" % t, [P, T], F32) for t in range(PACK)]
+        th = [sbt("th_%d" % t, [P, T], F32) for t in range(PACK)]
+        e_up = [sbt("e_up_%d" % t, [P, T], F32) for t in range(PACK)]
+        e_dn = [sbt("e_dn_%d" % t, [P, T], F32) for t in range(PACK)]
+        den = [sbt("den_%d" % t, [P, T], F32) for t in range(PACK)]
+        h_grouped = [sbt("h_grouped_%d" % b, [P, BANK * PACK], BF16) for b in range(2)]
+        h_q = [sbt("h_q_%d" % b, [P, BANK], U32) for b in range(2)]
+        h_s = [sbt("h_s_%d" % b, [P, BANK], U8) for b in range(2)]
+        root = [sbt("root_%d" % j, [P, PACK * P], F32) for j in range(PACK)]
+        frac = [sbt("frac_%d" % j, [P, PACK * P], F32) for j in range(PACK)]
+        u_planes = [sbt("u_planes_%d" % j, [P, PACK * P], BF16) for j in range(PACK)]
+        u_grouped = [sbt("u_grouped_%d" % j, [P, PACK * P], BF16) for j in range(PACK)]
+        u_q = [sbt("u_q_%d" % j, [P, P], U32) for j in range(PACK)]
+        u_s = [sbt("u_s_%d" % j, [P, P], U8) for j in range(PACK)]
+        o_bank = {}
+
+        def y_product(l):
+            for j in range(PACK):
+                y_val[l, j] = sb.tile([P, N], BF16, name="y_val", bufs=8, align_bytes=64)
+                nc.vector.tensor_tensor(out=y_val[l, j][:], in0=y_codes8[l][:, j * N:(j + 1) * N].bitcast(FP8),
+                                        in1=scale_bank[:], op=ALU.mult)
+
+        def y_turn(l):
+            for h in range(2):
+                turn_bank[l, h] = ps.tile([P, 2, 2, P], F32, name="turn_bank", bufs=2)
+                for jj in range(2):
+                    words = y_val[l, 2 * h + jj][:].bitcast(F32)
+                    for u in range(2):
+                        nc.tensor.transpose(turn_bank[l, h][:, jj, u, :], words[:, u:N // 2:2], ident[:])
+
+        def y_copy_out(l):
+            for h in range(2):
+                dst = y_turned[l][:, h * 1024:(h + 1) * 1024].bitcast(F32).rearrange("p (j r u) -> p j r u", j=2, u=2)
+                nc.scalar.copy(out=dst, in_=turn_bank[l, h][:].rearrange("p j u r -> p j r u"))
+
+        def v_group(l):
+            dst = v_grouped[l][:].rearrange("p (t q m j) -> p q t m j", t=PACK, m=2, j=PACK)
+            src = v_raw[l][:].rearrange("p j (q m t) -> p q t m j", m=2, t=PACK)
+            nc.scalar.copy(out=dst, in_=src)
+
+        def quant(codes, scales, src):
+            nc.vector.quantize_mx(out=codes[:].bitcast(FP8X4), scales=scales[:], in_=src[:])
+
+        def z_matmul(l, t):
+            z_bank[l, t] = ps.tile([P, BANK], F32, name="acc_bank", bufs=5)
+            cols = slice(t * P, (t + 1) * P)
+            nc.tensor.matmul_mx(out=z_bank[l, t][:], lhsT=v_q[l][:, cols].bitcast(FP8X4), lhsT_scale=v_s[l][:, cols],
+                                rhs=y_q[l][:].bitcast(FP8X4), rhs_scale=y_s[l][:], start=True, stop=True)
+
+        def z_first():
+            for t in range(PACK):
+                nc.scalar.activation(out=x[t][:], in_=z_bank[0, t][:], func=ACT.Copy, scale=weight[:, 0, t:t + 1])
+
+        def z_add(l, t):
+            nc.vector.scalar_tensor_tensor(out=x[t][:], in0=z_bank[l, t][:], scalar=weight[:, l, t:t + 1], in1=x[t][:],
+                                           op0=ALU.mult, op1=ALU.add)
+
+        def clamp(t):
+            nc.vector.tensor_scalar(out=x_cl[t][:], in0=x[t][:], scalar1=x_lo[:, t:t + 1], scalar2=x_hi[:, t:t + 1],
+                                    op0=ALU.max, op1=ALU.min)
+
+        def tanh_part(t):
+            nc.scalar.activation(out=th[t][:], in_=x[t][:], func=ACT.Tanh, scale=k1_sign[:, t:t + 1])
+
+        def exp_part(t):
+            nc.scalar.activation(out=e_up[t][:], in_=x_cl[t][:], func=ACT.Exp, scale=2.0, bias=log_ratio[:, t:t + 1])
+            nc.scalar.activation(out=e_dn[t][:], in_=x_cl[t][:], func=ACT.Exp, scale=-2.0, bias=log_ratio[:, t:t + 1])
+
+        def den_add(t):
+            nc.vector.scalar_tensor_tensor(out=den[t][:], in0=e_up[t][:], scalar=one_minus_ratio[:, t:t + 1], in1=e_dn[t][:],
+                                           op0=ALU.add, op1=ALU.add)
+
+        def h_group(b, on_vector):
+            dst = h_grouped[b][:].rearrange("p (c i j) -> p c j i", i=4, j=PACK)
+            src = h_raw[:, :, b * BANK:(b + 1) * BANK].rearrange("p j (c i) -> p c j i", i=4)
+            if on_vector:
+                nc.vector.tensor_copy(out=dst, in_=src)
+            else:
+                nc.scalar.copy(out=dst, in_=src)
+
+        def inverse(j):
+            for t in range(PACK):
+                nc.scalar.activation(out=root[j][:, t * P:(t + 1) * P], in_=den[t][:, j * P:(j + 1) * P],
+                                     func=ACT.Abs_reciprocal_sqrt, scale=inv_k1[:, t:t + 1])
+            nc.scalar.activation(out=frac[j][:], in_=root[j][:], func=ACT.Square)
+
+        def u_make(j):
+            for t in range(PACK):
+                nc.vector.scalar_tensor_tensor(out=u_planes[j][:, t * P:(t + 1) * P], in0=frac[j][:, t * P:(t + 1) * P],
+                                               scalar=k2_signed[:, t:t + 1], in1=th[t][:, j * P:(j + 1) * P],
+                                               op0=ALU.add, op1=ALU.mult)
+
+        def u_group(j, on_vector):
+            dst = u_grouped[j][:].rearrange("p (c i t) -> p c t i", i=4, t=PACK)
+            src = u_planes[j][:].rearrange("p (t c i) -> p c t i", i=4, t=PACK)
+            if on_vector:
+                nc.vector.tensor_copy(out=dst, in_=src)
+            else:
+                nc.scalar.copy(out=dst, in_=src)
+
+        def u_quant_matmul(j):
+            quant(u_q[j], u_s[j], u_grouped[j])
+            for b in range(2):
+                o_bank[j, b] = ps.tile([P, BANK], F32, name="acc_bank", bufs=5)
+                nc.tensor.matmul_mx(out=o_bank[j, b][:], lhsT=u_q[j][:].bitcast(FP8X4), lhsT_scale=u_s[j][:],
+                                    rhs=h_q[b][:].bitcast(FP8X4), rhs_scale=h_s[b][:], start=True, stop=True)
+
+        out_rows = out.rearrange("(r j) m -> j r m", j=PACK)
+
+        def finish(j):
+            for b in range(2):
+                res = sb.tile([P, BANK], F32, name="res", bufs=8, align_bytes=64)
+                cols = slice(b * BANK, (b + 1) * BANK)
+                nc.vector.tensor_tensor(out=res[:], in0=y0_sb[:, j, cols], in1=o_bank[j, b][:], op=ALU.subtract)
+                nc.sync.dma_start(out=out_rows[j][:, cols], in_=res[:])
+
+        y_product(0)
+        y_turn(0)
+        y_product(1)
+        v_group(0)
+        y_copy_out(0)
+        y_turn(1)
+        quant(v_q[0], v_s[0], v_grouped[0])
+        quant(y_q[0], y_s[0], y_turned[0])
+        for t in range(PACK):
+            z_matmul(0, t)
+        y_product(2)
+        v_group(1)
+        z_first()
+        quant(v_q[1], v_s[1], v_grouped[1])
+        y_copy_out(1)
+        y_turn(2)
+        y_product(3)
+        nc.vector.reciprocal(out=inv_k1[:], in_=k1_floor[:])
+        quant(y_q[1], y_s[1], y_turned[1])
+        for t in range(PACK):
+            z_matmul(1, t)
+        v_group(2)
+        quant(v_q[2], v_s[2], v_grouped[2])
+        y_copy_out(2)
+        y_turn(3)
+        z_add(1, 0)
+        z_add(1, 1)
+        quant(y_q[2], y_s[2], y_turned[2])
+        z_matmul(2, 0)
+        z_matmul(2, 1)
+        z_add(1, 2)
+        z_add(1, 3)
+        v_group(3)
+        quant(v_q[3], v_s[3], v_grouped[3])
+        y_copy_out(3)
+        h_group(0, False)
+        z_add(2, 0)
+        quant(y_q[3], y_s[3], y_turned[3])
+        z_matmul(3, 0)
+        z_matmul(2, 2)
+        z_matmul(3, 1)
+        z_matmul(2, 3)
+        z_add(2, 1)
+        z_matmul(3, 2)
+        z_add(3, 0)
+        z_matmul(3, 3)
+        tanh_part(0)
+        z_add(2, 2)
+        clamp(0)
+        exp_part(0)
+        z_add(3, 1)
+        tanh_part(1)
+        z_add(2, 3)
+        clamp(1)
+        exp_part(1)
+        z_add(3, 2)
+        tanh_part(2)
+        z_add(3, 3)
+        clamp(2)
+        exp_part(2)
+        tanh_part(3)
+        den_add(0)
+        clamp(3)
+        exp_part(3)
+        den_add(1)
+        quant(h_q[0], h_s[0], h_grouped[0])
+        den_add(2)
+        den_add(3)
+        h_group(1, True)
+
+        inverse(0)
+        u_make(0)
+        quant(h_q[1], h_s[1], h_grouped[1])
+        inverse(1)
+        u_group(0, True)
+        u_make(1)
+        inverse(2)
+        u_quant_matmul(0)
+        u_make(2)
+        u_group(1, False)
+        u_quant_matmul(1)
+        inverse(3)
+        finish(0)
+        u_make(3)
+        u_group(2, False)
+        u_quant_matmul(2)
+        u_group(3, False)
+        finish(1)
+        u_quant_matmul(3)
+        finish(2)
+        finish(3)

@@ -64,37 +64,37 @@ def tile_cellfreelsfdpaminterferenceresidual_kernel(tc, y_bytes, y_scale, v, a, 
         nc.vector.reciprocal(out=inv_nv[:], in_=nv_sb[:])
         ratio = par("ratio")
         nc.scalar.activation(out=ratio[:], in_=inv_nv[:], func=ACT.Exp, scale=-0.8)
+        log_ratio = par("log_ratio")
+        nc.scalar.activation(out=log_ratio[:], in_=inv_nv[:], func=ACT.Copy, scale=-0.8)
+        x_hi = par("x_hi")
+        nc.scalar.activation(out=x_hi[:], in_=inv_nv[:], func=ACT.Copy, scale=0.4, bias=EXP_CAP / 2)
+        x_lo = par("x_lo")
+        nc.scalar.activation(out=x_lo[:], in_=inv_nv[:], func=ACT.Copy, scale=-0.4, bias=-EXP_CAP / 2)
+        one_minus_ratio = par("one_minus_ratio")
+        nc.scalar.activation(out=one_minus_ratio[:], in_=ratio[:], func=ACT.Copy, scale=-1.0, bias=1.0)
+        k1_unit = par("k1_unit")
+        nc.scalar.activation(out=k1_unit[:], in_=ratio[:], func=ACT.Copy, scale=6.0 * C, bias=-2.0 * C)
         c_over_nv = par("c_over_nv")
         nc.gpsimd.tensor_scalar(out=c_over_nv[:], in0=inv_nv[:], scalar1=C, scalar2=0.0, op0=ALU.mult, op1=ALU.add)
         weight = sbt("weight", [P, L, PACK], F32)
         nc.gpsimd.tensor_tensor(out=weight[:], in0=a_sb[:], in1=c_over_nv[:].unsqueeze(1).to_broadcast([P, L, PACK]), op=ALU.mult)
-        log_ratio = par("log_ratio")
-        nc.gpsimd.tensor_scalar(out=log_ratio[:], in0=inv_nv[:], scalar1=-0.8, scalar2=0.0, op0=ALU.mult, op1=ALU.add)
-        x_hi = par("x_hi")
-        nc.gpsimd.tensor_scalar(out=x_hi[:], in0=inv_nv[:], scalar1=0.4, scalar2=EXP_CAP / 2, op0=ALU.mult, op1=ALU.add)
-        x_lo = par("x_lo")
-        nc.gpsimd.tensor_scalar(out=x_lo[:], in0=inv_nv[:], scalar1=-0.4, scalar2=-EXP_CAP / 2, op0=ALU.mult, op1=ALU.add)
-        one_minus_ratio = par("one_minus_ratio")
-        nc.gpsimd.tensor_scalar(out=one_minus_ratio[:], in0=ratio[:], scalar1=-1.0, scalar2=1.0, op0=ALU.mult, op1=ALU.add)
-        k1_unit = par("k1_unit")
-        nc.gpsimd.tensor_scalar(out=k1_unit[:], in0=ratio[:], scalar1=6.0 * C, scalar2=-2.0 * C, op0=ALU.mult, op1=ALU.add)
         k1 = par("k1")
-        nc.gpsimd.tensor_tensor(out=k1[:], in0=k1_unit[:], in1=g_sb[:], op=ALU.mult)
-        half_sign = par("half_sign")
-        nc.gpsimd.tensor_scalar(out=half_sign[:], in0=k1[:], scalar1=0.0, scalar2=0.5, op0=ALU.is_ge, op1=ALU.subtract)
         k1_sign = par("k1_sign")
-        nc.gpsimd.tensor_scalar(out=k1_sign[:], in0=half_sign[:], scalar1=2.0, scalar2=0.0, op0=ALU.mult, op1=ALU.add)
-        k1_abs = par("k1_abs")
-        nc.gpsimd.tensor_tensor(out=k1_abs[:], in0=k1[:], in1=k1_sign[:], op=ALU.mult)
-        k1_floor = par("k1_floor")
-        nc.gpsimd.tensor_scalar(out=k1_floor[:], in0=k1_abs[:], scalar1=1.0, scalar2=TINY, op0=ALU.mult, op1=ALU.max)
-        g_signed = par("g_signed")
-        nc.gpsimd.tensor_tensor(out=g_signed[:], in0=k1_sign[:], in1=g_sb[:], op=ALU.mult)
-        k2_signed = par("k2_signed")
-        nc.gpsimd.tensor_scalar(out=k2_signed[:], in0=g_signed[:], scalar1=3.0 * C, scalar2=0.0, op0=ALU.mult, op1=ALU.add)
+        k1_safe = par("k1_safe")
         inv_k1 = par("inv_k1")
+        k2_signed = par("k2_signed")
 
-        scale_bank = ps.tile([P, BANK], F32, name="scale_bank")
+        free_banks = list(range(8))
+        bank_of = {}
+
+        def take_bank(key, shape):
+            bank_of[key] = free_banks.pop(0)
+            return ps.tile(shape, F32, name="bank_%d" % bank_of[key])
+
+        def give_bank(key):
+            free_banks.append(bank_of[key])
+
+        scale_bank = take_bank("scale", [P, BANK])
         for t in range(PACK):
             nc.tensor.transpose(scale_bank[:, t:BANK:PACK], scale_col[:, t:t + 1].to_broadcast([P, P]), ident[:])
 
@@ -125,45 +125,58 @@ def tile_cellfreelsfdpaminterferenceresidual_kernel(tc, y_bytes, y_scale, v, a, 
         o_bank = {}
 
         def y_product(l):
-            for j in range(PACK):
-                y_val[l, j] = sb.tile([P, N], BF16, name="y_val", bufs=8, align_bytes=64)
-                nc.vector.tensor_tensor(out=y_val[l, j][:], in0=y_codes8[l][:, j * N:(j + 1) * N].bitcast(FP8),
-                                        in1=scale_bank[:], op=ALU.mult)
+            for h in range(2):
+                y_val[l, h] = sb.tile([P, 2 * N], BF16, name="y_val", bufs=4, align_bytes=64)
+                for jj in range(2):
+                    j = 2 * h + jj
+                    nc.vector.tensor_tensor(out=y_val[l, h][:, jj * N:(jj + 1) * N],
+                                            in0=y_codes8[l][:, j * N:(j + 1) * N].bitcast(FP8),
+                                            in1=scale_bank[:], op=ALU.mult)
+            if l == L - 1:
+                give_bank("scale")
 
         def y_turn(l):
             for h in range(2):
-                turn_bank[l, h] = ps.tile([P, 2, 2, P], F32, name="turn_bank", bufs=2)
+                turn_bank[l, h] = take_bank(("turn", l, h), [P, 2, 2, P])
+                words = y_val[l, h][:].bitcast(F32)
                 for jj in range(2):
-                    words = y_val[l, 2 * h + jj][:].bitcast(F32)
                     for u in range(2):
-                        nc.tensor.transpose(turn_bank[l, h][:, jj, u, :], words[:, u:N // 2:2], ident[:])
+                        first = jj * (N // 2) + u
+                        nc.tensor.transpose(turn_bank[l, h][:, jj, u, :], words[:, first:(jj + 1) * (N // 2):2], ident[:])
 
         def y_copy_out(l):
             for h in range(2):
                 dst = y_turned[l][:, h * 1024:(h + 1) * 1024].bitcast(F32).rearrange("p (j r u) -> p j r u", j=2, u=2)
                 nc.scalar.copy(out=dst, in_=turn_bank[l, h][:].rearrange("p j u r -> p j r u"))
+                give_bank(("turn", l, h))
 
-        def v_group(l):
-            dst = v_grouped[l][:].rearrange("p (t q m j) -> p q t m j", t=PACK, m=2, j=PACK)
-            src = v_raw[l][:].rearrange("p j (q m t) -> p q t m j", m=2, t=PACK)
+        def v_scalar(l):
+            dst = v_grouped[l][:, 0:1024].rearrange("p (t q m j) -> p q j m t", t=2, m=2, j=PACK)
+            src = v_raw[l][:].rearrange("p j (q m t) -> p q j m t", m=2, t=PACK)[:, :, :, :, 0:2]
             nc.scalar.copy(out=dst, in_=src)
+
+        def v_gpsimd(l):
+            dst = v_grouped[l][:, 1024:2048].rearrange("p (t m j) -> p t m j", t=2, j=PACK)
+            src = v_raw[l][:].rearrange("p j (m t) -> p t m j", t=PACK)[:, 2:4]
+            nc.gpsimd.tensor_scalar(out=dst, in0=src, scalar1=1.0, scalar2=0.0, op0=ALU.mult, op1=ALU.add)
 
         def quant(codes, scales, src):
             nc.vector.quantize_mx(out=codes[:].bitcast(FP8X4), scales=scales[:], in_=src[:])
 
         def z_matmul(l, t):
-            z_bank[l, t] = ps.tile([P, BANK], F32, name="acc_bank", bufs=5)
+            z_bank[l, t] = take_bank(("z", l, t), [P, BANK])
             cols = slice(t * P, (t + 1) * P)
             nc.tensor.matmul_mx(out=z_bank[l, t][:], lhsT=v_q[l][:, cols].bitcast(FP8X4), lhsT_scale=v_s[l][:, cols],
                                 rhs=y_q[l][:].bitcast(FP8X4), rhs_scale=y_s[l][:], start=True, stop=True)
 
-        def z_first():
-            for t in range(PACK):
-                nc.scalar.activation(out=x[t][:], in_=z_bank[0, t][:], func=ACT.Copy, scale=weight[:, 0, t:t + 1])
+        def z_first(t):
+            nc.scalar.activation(out=x[t][:], in_=z_bank[0, t][:], func=ACT.Copy, scale=weight[:, 0, t:t + 1])
+            give_bank(("z", 0, t))
 
         def z_add(l, t):
             nc.vector.scalar_tensor_tensor(out=x[t][:], in0=z_bank[l, t][:], scalar=weight[:, l, t:t + 1], in1=x[t][:],
                                            op0=ALU.mult, op1=ALU.add)
+            give_bank(("z", l, t))
 
         def clamp(t):
             nc.vector.tensor_scalar(out=x_cl[t][:], in0=x[t][:], scalar1=x_lo[:, t:t + 1], scalar2=x_hi[:, t:t + 1],
@@ -180,9 +193,9 @@ def tile_cellfreelsfdpaminterferenceresidual_kernel(tc, y_bytes, y_scale, v, a, 
             nc.vector.scalar_tensor_tensor(out=den[t][:], in0=e_up[t][:], scalar=one_minus_ratio[:, t:t + 1], in1=e_dn[t][:],
                                            op0=ALU.add, op1=ALU.add)
 
-        def h_group(b, on_vector):
-            dst = h_grouped[b][:].rearrange("p (c i j) -> p c j i", i=4, j=PACK)
-            src = h_raw[:, :, b * BANK:(b + 1) * BANK].rearrange("p j (c i) -> p c j i", i=4)
+        def h_part(b, s, on_vector):
+            dst = h_grouped[b][:, s * 1024:(s + 1) * 1024].rearrange("p (c i j) -> p c j i", i=4, j=PACK)
+            src = h_raw[:, :, b * BANK + s * 256:b * BANK + (s + 1) * 256].rearrange("p j (c i) -> p c j i", i=4)
             if on_vector:
                 nc.vector.tensor_copy(out=dst, in_=src)
             else:
@@ -211,7 +224,7 @@ def tile_cellfreelsfdpaminterferenceresidual_kernel(tc, y_bytes, y_scale, v, a, 
         def u_quant_matmul(j):
             quant(u_q[j], u_s[j], u_grouped[j])
             for b in range(2):
-                o_bank[j, b] = ps.tile([P, BANK], F32, name="acc_bank", bufs=5)
+                o_bank[j, b] = take_bank(("o", j, b), [P, BANK])
                 nc.tensor.matmul_mx(out=o_bank[j, b][:], lhsT=u_q[j][:].bitcast(FP8X4), lhsT_scale=u_s[j][:],
                                     rhs=h_q[b][:].bitcast(FP8X4), rhs_scale=h_s[b][:], start=True, stop=True)
 
@@ -222,81 +235,85 @@ def tile_cellfreelsfdpaminterferenceresidual_kernel(tc, y_bytes, y_scale, v, a, 
                 res = sb.tile([P, BANK], F32, name="res", bufs=8, align_bytes=64)
                 cols = slice(b * BANK, (b + 1) * BANK)
                 nc.vector.tensor_tensor(out=res[:], in0=y0_sb[:, j, cols], in1=o_bank[j, b][:], op=ALU.subtract)
+                give_bank(("o", j, b))
                 nc.sync.dma_start(out=out_rows[j][:, cols], in_=res[:])
 
-        y_product(0)
-        y_turn(0)
-        y_product(1)
-        v_group(0)
-        y_copy_out(0)
-        y_turn(1)
+        for l in range(L):
+            y_product(l)
+            y_turn(l)
+            v_scalar(l)
+            v_gpsimd(l)
+            if l > 0:
+                y_copy_out(l - 1)
+        nc.gpsimd.tensor_tensor(out=k1[:], in0=k1_unit[:], in1=g_sb[:], op=ALU.mult)
         quant(v_q[0], v_s[0], v_grouped[0])
         quant(y_q[0], y_s[0], y_turned[0])
-        for t in range(PACK):
-            z_matmul(0, t)
-        y_product(2)
-        v_group(1)
-        z_first()
+        y_copy_out(3)
+        z_matmul(0, 0)
+        z_matmul(0, 1)
         quant(v_q[1], v_s[1], v_grouped[1])
-        y_copy_out(1)
-        y_turn(2)
-        y_product(3)
-        nc.vector.reciprocal(out=inv_k1[:], in_=k1_floor[:])
         quant(y_q[1], y_s[1], y_turned[1])
+        z_matmul(1, 0)
+        z_matmul(0, 2)
+        z_matmul(0, 3)
+        nc.scalar.activation(out=k1_sign[:], in_=k1[:], func=ACT.Sign)
+        nc.scalar.activation(out=k1_safe[:], in_=k1[:], func=ACT.Copy, scale=1.0, bias=TINY)
+        h_part(0, 0, False)
         for t in range(PACK):
-            z_matmul(1, t)
-        v_group(2)
+            z_first(t)
+        h_part(0, 1, False)
         quant(v_q[2], v_s[2], v_grouped[2])
-        y_copy_out(2)
-        y_turn(3)
-        z_add(1, 0)
-        z_add(1, 1)
         quant(y_q[2], y_s[2], y_turned[2])
         z_matmul(2, 0)
-        z_matmul(2, 1)
-        z_add(1, 2)
-        z_add(1, 3)
-        v_group(3)
+        z_matmul(1, 1)
         quant(v_q[3], v_s[3], v_grouped[3])
-        y_copy_out(3)
-        h_group(0, False)
-        z_add(2, 0)
         quant(y_q[3], y_s[3], y_turned[3])
         z_matmul(3, 0)
-        z_matmul(2, 2)
+        z_matmul(2, 1)
         z_matmul(3, 1)
-        z_matmul(2, 3)
-        z_add(2, 1)
+        z_matmul(1, 2)
+        z_add(1, 0)
+        z_matmul(2, 2)
+        z_add(1, 1)
         z_matmul(3, 2)
+        z_add(2, 0)
+        z_matmul(1, 3)
+        z_add(2, 1)
+        z_matmul(2, 3)
         z_add(3, 0)
         z_matmul(3, 3)
         tanh_part(0)
-        z_add(2, 2)
+        z_add(3, 1)
         clamp(0)
         exp_part(0)
-        z_add(3, 1)
         tanh_part(1)
-        z_add(2, 3)
+        z_add(1, 2)
         clamp(1)
         exp_part(1)
+        z_add(2, 2)
+        z_add(1, 3)
         z_add(3, 2)
         tanh_part(2)
-        z_add(3, 3)
+        z_add(2, 3)
         clamp(2)
         exp_part(2)
+        z_add(3, 3)
         tanh_part(3)
-        den_add(0)
+        nc.vector.reciprocal(out=inv_k1[:], in_=k1_safe[:])
         clamp(3)
         exp_part(3)
+        den_add(0)
         den_add(1)
-        quant(h_q[0], h_s[0], h_grouped[0])
+        h_part(1, 0, True)
         den_add(2)
+        nc.vector.scalar_tensor_tensor(out=k2_signed[:], in0=g_sb[:], scalar=3.0 * C, in1=k1_sign[:], op0=ALU.mult, op1=ALU.mult)
         den_add(3)
-        h_group(1, True)
+        h_part(1, 1, True)
+        quant(h_q[0], h_s[0], h_grouped[0])
+        quant(h_q[1], h_s[1], h_grouped[1])
 
         inverse(0)
         u_make(0)
-        quant(h_q[1], h_s[1], h_grouped[1])
         inverse(1)
         u_group(0, True)
         u_make(1)

@@ -19,9 +19,15 @@ ACT = mybir.ActivationFunctionType
 P = 128
 PACK = 4
 BANK = 512
+PSUM_BANKS = 8
+HALF = 1024
+OUT_BLOCKS = M // BANK
 C = 1.0 / math.sqrt(5.0)
 EXP_CAP = 40.0
 TINY = 2.0 ** -60
+GPSIMD_POINTS = 3
+VECTOR_GROUPS = 2
+FINISH_LAG = 3
 
 
 def tile_cellfreelsfdpaminterferenceresidual_kernel(tc, y_bytes, y_scale, v, a, nv, g, h0, y0, out):
@@ -31,98 +37,99 @@ def tile_cellfreelsfdpaminterferenceresidual_kernel(tc, y_bytes, y_scale, v, a, 
         ps = ctx.enter_context(tc.psum_pool(name="ps", bufs=1))
         ctx.enter_context(tc.manual_schedule())
 
-        def sbt(name, shape, dtype):
+        def sbuf(name, shape, dtype):
             return sb.tile(shape, dtype, name=name, align_bytes=64)
 
-        scale_col = sbt("scale_col", [P, PACK], F32)
+        def sbuf_list(name, count, shape, dtype):
+            return [sbuf("%s_%d" % (name, i), shape, dtype) for i in range(count)]
+
+        scale_col = sbuf("scale_col", [P, PACK], F32)
         nc.sync.dma_start(out=scale_col[:], in_=y_scale.rearrange("a b (p t) -> p (a b t)", t=PACK))
-        nv_sb = sbt("nv_sb", [P, PACK], BF16)
-        a_sb = sbt("a_sb", [P, L, PACK], BF16)
-        g_sb = sbt("g_sb", [P, PACK], BF16)
+        nv_sb = sbuf("nv_sb", [P, PACK], BF16)
+        a_sb = sbuf("a_sb", [P, L, PACK], BF16)
+        g_sb = sbuf("g_sb", [P, PACK], BF16)
         nc.scalar.dma_start(out=nv_sb[:], in_=nv.rearrange("(p t) -> p t", t=PACK))
         nc.scalar.dma_start(out=a_sb[:], in_=a.rearrange("l (p t) -> p l t", t=PACK))
         nc.scalar.dma_start(out=g_sb[:], in_=g.rearrange("(p t) -> p t", t=PACK))
-        y_codes8 = []
-        v_raw = []
+        y_fp8 = sbuf_list("y_fp8", L, [P, PACK * N], U8)
+        v_raw = sbuf_list("v_raw", L, [P, PACK, K], BF16)
         for l in range(L):
-            y_codes8.append(sbt("y_fp8_%d" % l, [P, PACK * N], U8))
-            v_raw.append(sbt("v_raw_%d" % l, [P, PACK, K], BF16))
-            nc.sync.dma_start(out=y_codes8[l][:], in_=y_bytes[l].rearrange("(p j) n -> p (j n)", j=PACK))
-            nc.sync.dma_start(out=v_raw[l][:], in_=v[l].rearrange("(p j) k -> p j k", j=PACK))
-        h_raw = sbt("h_raw", [P, PACK, M], BF16)
-        nc.sync.dma_start(out=h_raw[:], in_=h0.rearrange("(p j) m -> p j m", j=PACK))
-        y0_sb = sbt("y0_sb", [P, PACK, M], BF16)
-        nc.sync.dma_start(out=y0_sb[:], in_=y0.rearrange("(p j) m -> p j m", j=PACK))
+            nc.sync.dma_start(out=y_fp8[l][:], in_=y_bytes[l].rearrange("(r j) n -> r (j n)", j=PACK))
+            nc.sync.dma_start(out=v_raw[l][:], in_=v[l].rearrange("(p i) k -> p i k", i=PACK))
+        h_raw = sbuf("h_raw", [P, PACK, M], BF16)
+        nc.sync.dma_start(out=h_raw[:], in_=h0.rearrange("(p t) m -> p t m", t=PACK))
+        y0_sb = sbuf("y0_sb", [P, PACK, M], BF16)
+        nc.sync.dma_start(out=y0_sb[:], in_=y0.rearrange("(r j) m -> r j m", j=PACK))
 
-        ident = sbt("ident", [P, P], F32)
+        ident = sbuf("ident", [P, P], F32)
         make_identity(nc, ident[:])
 
-        def par(name):
-            return sbt(name, [P, PACK], F32)
+        def channel_tile(name):
+            return sbuf(name, [P, PACK], F32)
 
-        inv_nv = par("inv_nv")
+        def affine(name, src, scale, bias):
+            dst = channel_tile(name)
+            nc.scalar.activation(out=dst[:], in_=src[:], func=ACT.Copy, scale=scale, bias=bias)
+            return dst
+
+        inv_nv = channel_tile("inv_nv")
         nc.vector.reciprocal(out=inv_nv[:], in_=nv_sb[:])
-        ratio = par("ratio")
+        ratio = channel_tile("ratio")
         nc.scalar.activation(out=ratio[:], in_=inv_nv[:], func=ACT.Exp, scale=-0.8)
-        log_ratio = par("log_ratio")
-        nc.scalar.activation(out=log_ratio[:], in_=inv_nv[:], func=ACT.Copy, scale=-0.8)
-        x_hi = par("x_hi")
-        nc.scalar.activation(out=x_hi[:], in_=inv_nv[:], func=ACT.Copy, scale=0.4, bias=EXP_CAP / 2)
-        x_lo = par("x_lo")
-        nc.scalar.activation(out=x_lo[:], in_=inv_nv[:], func=ACT.Copy, scale=-0.4, bias=-EXP_CAP / 2)
-        one_minus_ratio = par("one_minus_ratio")
-        nc.scalar.activation(out=one_minus_ratio[:], in_=ratio[:], func=ACT.Copy, scale=-1.0, bias=1.0)
-        k1_unit = par("k1_unit")
-        nc.scalar.activation(out=k1_unit[:], in_=ratio[:], func=ACT.Copy, scale=6.0 * C, bias=-2.0 * C)
-        c_over_nv = par("c_over_nv")
+        log_ratio = affine("log_ratio", inv_nv, -0.8, 0.0)
+        x_hi = affine("x_hi", inv_nv, 0.4, EXP_CAP / 2)
+        x_lo = affine("x_lo", inv_nv, -0.4, -EXP_CAP / 2)
+        one_minus_ratio = affine("one_minus_ratio", ratio, -1.0, 1.0)
+        k1_over_g = affine("k1_over_g", ratio, 6.0 * C, -2.0 * C)
+        c_over_nv = channel_tile("c_over_nv")
         nc.gpsimd.tensor_scalar(out=c_over_nv[:], in0=inv_nv[:], scalar1=C, scalar2=0.0, op0=ALU.mult, op1=ALU.add)
-        weight = sbt("weight", [P, L, PACK], F32)
-        nc.gpsimd.tensor_tensor(out=weight[:], in0=a_sb[:], in1=c_over_nv[:].unsqueeze(1).to_broadcast([P, L, PACK]), op=ALU.mult)
-        k1 = par("k1")
-        k1_sign = par("k1_sign")
-        k1_safe = par("k1_safe")
-        inv_k1 = par("inv_k1")
-        k2_signed = par("k2_signed")
+        weight = sbuf("weight", [P, L, PACK], F32)
+        nc.gpsimd.tensor_tensor(out=weight[:], in0=a_sb[:],
+                                in1=c_over_nv[:].unsqueeze(1).to_broadcast([P, L, PACK]), op=ALU.mult)
+        k1 = channel_tile("k1")
+        k1_sign = channel_tile("k1_sign")
+        k1_safe = channel_tile("k1_safe")
+        inv_k1 = channel_tile("inv_k1")
+        k2_signed = channel_tile("k2_signed")
 
-        free_banks = list(range(8))
+        free_banks = list(range(PSUM_BANKS))
         bank_of = {}
+        psum = {}
 
         def take_bank(key, shape):
             bank_of[key] = free_banks.pop(0)
-            return ps.tile(shape, F32, name="bank_%d" % bank_of[key])
+            psum[key] = ps.tile(shape, F32, name="bank_%d" % bank_of[key])
+            return psum[key]
 
         def give_bank(key):
             free_banks.append(bank_of[key])
 
-        scale_bank = take_bank("scale", [P, BANK])
+        scale_bank = take_bank("scale", [P, N])
         for t in range(PACK):
-            nc.tensor.transpose(scale_bank[:, t:BANK:PACK], scale_col[:, t:t + 1].to_broadcast([P, P]), ident[:])
+            nc.tensor.transpose(scale_bank[:, t:N:PACK], scale_col[:, t:t + 1].to_broadcast([P, P]), ident[:])
 
         y_val = {}
-        turn_bank = {}
-        y_turned = [sbt("y_turned_%d" % l, [P, T * PACK], BF16) for l in range(L)]
-        v_grouped = [sbt("v_grouped_%d" % l, [P, K * PACK], BF16) for l in range(L)]
-        y_q = [sbt("y_q_%d" % l, [P, T], U32) for l in range(L)]
-        y_s = [sbt("y_s_%d" % l, [P, T], U8) for l in range(L)]
-        v_q = [sbt("v_q_%d" % l, [P, K], U32) for l in range(L)]
-        v_s = [sbt("v_s_%d" % l, [P, K], U8) for l in range(L)]
-        z_bank = {}
-        x = [sbt("x_%d" % t, [P, T], F32) for t in range(PACK)]
-        x_cl = [sbt("x_cl_%d" % t, [P, T], F32) for t in range(PACK)]
-        th = [sbt("th_%d" % t, [P, T], F32) for t in range(PACK)]
-        e_up = [sbt("e_up_%d" % t, [P, T], F32) for t in range(PACK)]
-        e_dn = [sbt("e_dn_%d" % t, [P, T], F32) for t in range(PACK)]
-        den = [sbt("den_%d" % t, [P, T], F32) for t in range(PACK)]
-        h_grouped = [sbt("h_grouped_%d" % b, [P, BANK * PACK], BF16) for b in range(2)]
-        h_q = [sbt("h_q_%d" % b, [P, BANK], U32) for b in range(2)]
-        h_s = [sbt("h_s_%d" % b, [P, BANK], U8) for b in range(2)]
-        root = [sbt("root_%d" % j, [P, PACK * P], F32) for j in range(PACK)]
-        frac = [sbt("frac_%d" % j, [P, PACK * P], F32) for j in range(PACK)]
-        u_planes = [sbt("u_planes_%d" % j, [P, PACK * P], BF16) for j in range(PACK)]
-        u_grouped = [sbt("u_grouped_%d" % j, [P, PACK * P], BF16) for j in range(PACK)]
-        u_q = [sbt("u_q_%d" % j, [P, P], U32) for j in range(PACK)]
-        u_s = [sbt("u_s_%d" % j, [P, P], U8) for j in range(PACK)]
-        o_bank = {}
+        y_grouped = sbuf_list("y_grouped", L, [P, T * PACK], BF16)
+        v_grouped = sbuf_list("v_grouped", L, [P, K * PACK], BF16)
+        y_codes = sbuf_list("y_codes", L, [P, T], U32)
+        y_scales = sbuf_list("y_scales", L, [P, T], U8)
+        v_codes = sbuf_list("v_codes", L, [P, K], U32)
+        v_scales = sbuf_list("v_scales", L, [P, K], U8)
+        x = sbuf_list("x", PACK, [P, T], F32)
+        x_clamped = sbuf_list("x_clamped", PACK, [P, T], F32)
+        tanh_x = sbuf_list("tanh_x", PACK, [P, T], F32)
+        exp_up = sbuf_list("exp_up", PACK, [P, T], F32)
+        exp_down = sbuf_list("exp_down", PACK, [P, T], F32)
+        denom = sbuf_list("denom", PACK, [P, T], F32)
+        h_grouped = sbuf_list("h_grouped", OUT_BLOCKS, [P, BANK * PACK], BF16)
+        h_codes = sbuf_list("h_codes", OUT_BLOCKS, [P, BANK], U32)
+        h_scales = sbuf_list("h_scales", OUT_BLOCKS, [P, BANK], U8)
+        root = sbuf_list("root", PACK, [P, PACK * P], F32)
+        frac = sbuf_list("frac", PACK, [P, PACK * P], F32)
+        u_tiles = sbuf_list("u_tiles", PACK, [P, PACK * P], BF16)
+        u_grouped = sbuf_list("u_grouped", PACK, [P, PACK * P], BF16)
+        u_codes = sbuf_list("u_codes", PACK, [P, P], U32)
+        u_scales = sbuf_list("u_scales", PACK, [P, P], U8)
 
         def y_product(l):
             for h in range(2):
@@ -130,205 +137,184 @@ def tile_cellfreelsfdpaminterferenceresidual_kernel(tc, y_bytes, y_scale, v, a, 
                 for jj in range(2):
                     j = 2 * h + jj
                     nc.vector.tensor_tensor(out=y_val[l, h][:, jj * N:(jj + 1) * N],
-                                            in0=y_codes8[l][:, j * N:(j + 1) * N].bitcast(FP8),
+                                            in0=y_fp8[l][:, j * N:(j + 1) * N].bitcast(FP8),
                                             in1=scale_bank[:], op=ALU.mult)
-            if l == L - 1:
-                give_bank("scale")
 
-        def y_turn(l):
+        def y_transpose(l):
             for h in range(2):
-                turn_bank[l, h] = take_bank(("turn", l, h), [P, 2, 2, P])
+                bank = take_bank(("turn", l, h), [P, 2, 2, P])
                 words = y_val[l, h][:].bitcast(F32)
                 for jj in range(2):
-                    for u in range(2):
-                        first = jj * (N // 2) + u
-                        nc.tensor.transpose(turn_bank[l, h][:, jj, u, :], words[:, first:(jj + 1) * (N // 2):2], ident[:])
+                    for e in range(2):
+                        first = jj * (N // 2) + e
+                        nc.tensor.transpose(bank[:, jj, e, :], words[:, first:(jj + 1) * (N // 2):2], ident[:])
 
         def y_copy_out(l):
             for h in range(2):
-                dst = y_turned[l][:, h * 1024:(h + 1) * 1024].bitcast(F32).rearrange("p (j r u) -> p j r u", j=2, u=2)
-                nc.scalar.copy(out=dst, in_=turn_bank[l, h][:].rearrange("p j u r -> p j r u"))
+                dst = y_grouped[l][:, h * HALF:(h + 1) * HALF].bitcast(F32)
+                nc.scalar.copy(out=dst.rearrange("p (j r e) -> p j r e", j=2, e=2),
+                               in_=psum["turn", l, h][:].rearrange("p j e r -> p j r e"))
                 give_bank(("turn", l, h))
 
-        def v_scalar(l):
-            dst = v_grouped[l][:, 0:1024].rearrange("p (t q m j) -> p q j m t", t=2, m=2, j=PACK)
-            src = v_raw[l][:].rearrange("p j (q m t) -> p q j m t", m=2, t=PACK)[:, :, :, :, 0:2]
+        def v_group_scalar(l, h):
+            dst = v_grouped[l][:, h * HALF:(h + 1) * HALF].rearrange("p (t w q i) -> p w t q i", t=2, q=2, i=PACK)
+            src = v_raw[l][:].rearrange("p i (w q t) -> p w t q i", q=2, t=PACK)[:, :, 2 * h:2 * h + 2]
             nc.scalar.copy(out=dst, in_=src)
 
-        def v_gpsimd(l):
-            dst = v_grouped[l][:, 1024:2048].rearrange("p (t m j) -> p t m j", t=2, j=PACK)
-            src = v_raw[l][:].rearrange("p j (m t) -> p t m j", t=PACK)[:, 2:4]
+        def v_group_gpsimd(l):
+            dst = v_grouped[l][:, HALF:2 * HALF].rearrange("p (t q i) -> p t q i", t=2, i=PACK)
+            src = v_raw[l][:].rearrange("p i (q t) -> p t q i", t=PACK)[:, 2:4]
             nc.gpsimd.tensor_scalar(out=dst, in0=src, scalar1=1.0, scalar2=0.0, op0=ALU.mult, op1=ALU.add)
 
-        def quant(codes, scales, src):
-            nc.vector.quantize_mx(out=codes[:].bitcast(FP8X4), scales=scales[:], in_=src[:])
+        def group(copy, dst, src):
+            copy(out=dst.rearrange("p (w col t) -> p w t col", col=4, t=PACK),
+                 in_=src.rearrange("p t (w col) -> p w t col", col=4))
+
+        def h_group(copy, b, h):
+            first = b * BANK + h * (BANK // 2)
+            group(copy, h_grouped[b][:, h * HALF:(h + 1) * HALF], h_raw[:, :, first:first + BANK // 2])
+
+        def quantize(codes, scales, grouped):
+            nc.vector.quantize_mx(out=codes[:].bitcast(FP8X4), scales=scales[:], in_=grouped[:])
 
         def z_matmul(l, t):
-            z_bank[l, t] = take_bank(("z", l, t), [P, BANK])
             cols = slice(t * P, (t + 1) * P)
-            nc.tensor.matmul_mx(out=z_bank[l, t][:], lhsT=v_q[l][:, cols].bitcast(FP8X4), lhsT_scale=v_s[l][:, cols],
-                                rhs=y_q[l][:].bitcast(FP8X4), rhs_scale=y_s[l][:], start=True, stop=True)
+            nc.tensor.matmul_mx(out=take_bank(("z", l, t), [P, T])[:],
+                                lhsT=v_codes[l][:, cols].bitcast(FP8X4), lhsT_scale=v_scales[l][:, cols],
+                                rhs=y_codes[l][:].bitcast(FP8X4), rhs_scale=y_scales[l][:], start=True, stop=True)
 
         def z_first(t):
-            nc.scalar.activation(out=x[t][:], in_=z_bank[0, t][:], func=ACT.Copy, scale=weight[:, 0, t:t + 1])
+            nc.scalar.activation(out=x[t][:], in_=psum["z", 0, t][:], func=ACT.Copy, scale=weight[:, 0, t:t + 1])
             give_bank(("z", 0, t))
 
         def z_add(l, t):
-            nc.vector.scalar_tensor_tensor(out=x[t][:], in0=z_bank[l, t][:], scalar=weight[:, l, t:t + 1], in1=x[t][:],
-                                           op0=ALU.mult, op1=ALU.add)
+            nc.vector.scalar_tensor_tensor(out=x[t][:], in0=psum["z", l, t][:], scalar=weight[:, l, t:t + 1],
+                                           in1=x[t][:], op0=ALU.mult, op1=ALU.add)
             give_bank(("z", l, t))
 
-        def clamp(t):
-            nc.vector.tensor_scalar(out=x_cl[t][:], in0=x[t][:], scalar1=x_lo[:, t:t + 1], scalar2=x_hi[:, t:t + 1],
-                                    op0=ALU.max, op1=ALU.min)
-
         def tanh_part(t):
-            nc.scalar.activation(out=th[t][:], in_=x[t][:], func=ACT.Tanh, scale=k1_sign[:, t:t + 1])
+            nc.scalar.activation(out=tanh_x[t][:], in_=x[t][:], func=ACT.Tanh, scale=k1_sign[:, t:t + 1])
 
-        def exp_part(t):
-            nc.scalar.activation(out=e_up[t][:], in_=x_cl[t][:], func=ACT.Exp, scale=2.0, bias=log_ratio[:, t:t + 1])
-            nc.scalar.activation(out=e_dn[t][:], in_=x_cl[t][:], func=ACT.Exp, scale=-2.0, bias=log_ratio[:, t:t + 1])
+        def clamp_and_exp(t):
+            nc.vector.tensor_scalar(out=x_clamped[t][:], in0=x[t][:], scalar1=x_lo[:, t:t + 1],
+                                    scalar2=x_hi[:, t:t + 1], op0=ALU.max, op1=ALU.min)
+            for dst, scale in ((exp_up, 2.0), (exp_down, -2.0)):
+                nc.scalar.activation(out=dst[t][:], in_=x_clamped[t][:], func=ACT.Exp, scale=scale,
+                                     bias=log_ratio[:, t:t + 1])
 
-        def den_add(t):
-            nc.vector.scalar_tensor_tensor(out=den[t][:], in0=e_up[t][:], scalar=one_minus_ratio[:, t:t + 1], in1=e_dn[t][:],
-                                           op0=ALU.add, op1=ALU.add)
+        def denom_sum(t):
+            nc.vector.scalar_tensor_tensor(out=denom[t][:], in0=exp_up[t][:], scalar=one_minus_ratio[:, t:t + 1],
+                                           in1=exp_down[t][:], op0=ALU.add, op1=ALU.add)
 
-        def h_part(b, s, on_vector):
-            dst = h_grouped[b][:, s * 1024:(s + 1) * 1024].rearrange("p (c i j) -> p c j i", i=4, j=PACK)
-            src = h_raw[:, :, b * BANK + s * 256:b * BANK + (s + 1) * 256].rearrange("p j (c i) -> p c j i", i=4)
-            if on_vector:
-                nc.vector.tensor_copy(out=dst, in_=src)
-            else:
-                nc.scalar.copy(out=dst, in_=src)
+        def inverse_root(j, t):
+            nc.scalar.activation(out=root[j][:, t * P:(t + 1) * P], in_=denom[t][:, j * P:(j + 1) * P],
+                                 func=ACT.Abs_reciprocal_sqrt, scale=inv_k1[:, t:t + 1])
 
-        def inverse(j):
-            for t in range(PACK):
-                nc.scalar.activation(out=root[j][:, t * P:(t + 1) * P], in_=den[t][:, j * P:(j + 1) * P],
-                                     func=ACT.Abs_reciprocal_sqrt, scale=inv_k1[:, t:t + 1])
-            nc.scalar.activation(out=frac[j][:], in_=root[j][:], func=ACT.Square)
+        def square(j, t):
+            nc.scalar.activation(out=frac[j][:, t * P:(t + 1) * P], in_=root[j][:, t * P:(t + 1) * P], func=ACT.Square)
 
         def u_make(j):
             for t in range(PACK):
-                nc.vector.scalar_tensor_tensor(out=u_planes[j][:, t * P:(t + 1) * P], in0=frac[j][:, t * P:(t + 1) * P],
-                                               scalar=k2_signed[:, t:t + 1], in1=th[t][:, j * P:(j + 1) * P],
+                nc.vector.scalar_tensor_tensor(out=u_tiles[j][:, t * P:(t + 1) * P], in0=frac[j][:, t * P:(t + 1) * P],
+                                               scalar=k2_signed[:, t:t + 1], in1=tanh_x[t][:, j * P:(j + 1) * P],
                                                op0=ALU.add, op1=ALU.mult)
 
-        def u_group(j, on_vector):
-            dst = u_grouped[j][:].rearrange("p (c i t) -> p c t i", i=4, t=PACK)
-            src = u_planes[j][:].rearrange("p (t c i) -> p c t i", i=4, t=PACK)
-            if on_vector:
-                nc.vector.tensor_copy(out=dst, in_=src)
-            else:
-                nc.scalar.copy(out=dst, in_=src)
+        def u_group(j):
+            copy = nc.vector.tensor_copy if j < VECTOR_GROUPS else nc.scalar.copy
+            group(copy, u_grouped[j][:], u_tiles[j][:].rearrange("p (t r) -> p t r", t=PACK))
 
-        def u_quant_matmul(j):
-            quant(u_q[j], u_s[j], u_grouped[j])
-            for b in range(2):
-                o_bank[j, b] = take_bank(("o", j, b), [P, BANK])
-                nc.tensor.matmul_mx(out=o_bank[j, b][:], lhsT=u_q[j][:].bitcast(FP8X4), lhsT_scale=u_s[j][:],
-                                    rhs=h_q[b][:].bitcast(FP8X4), rhs_scale=h_s[b][:], start=True, stop=True)
+        def u_quantize_and_matmul(j):
+            quantize(u_codes[j], u_scales[j], u_grouped[j])
+            for b in range(OUT_BLOCKS):
+                nc.tensor.matmul_mx(out=take_bank(("out", j, b), [P, BANK])[:],
+                                    lhsT=u_codes[j][:].bitcast(FP8X4), lhsT_scale=u_scales[j][:],
+                                    rhs=h_codes[b][:].bitcast(FP8X4), rhs_scale=h_scales[b][:], start=True, stop=True)
 
         out_rows = out.rearrange("(r j) m -> j r m", j=PACK)
 
         def finish(j):
-            for b in range(2):
-                res = sb.tile([P, BANK], F32, name="res", bufs=8, align_bytes=64)
+            for b in range(OUT_BLOCKS):
+                res = sb.tile([P, BANK], F32, name="res", bufs=PACK * OUT_BLOCKS, align_bytes=64)
                 cols = slice(b * BANK, (b + 1) * BANK)
-                nc.vector.tensor_tensor(out=res[:], in0=y0_sb[:, j, cols], in1=o_bank[j, b][:], op=ALU.subtract)
-                give_bank(("o", j, b))
+                nc.vector.tensor_tensor(out=res[:], in0=y0_sb[:, j, cols], in1=psum["out", j, b][:], op=ALU.subtract)
+                give_bank(("out", j, b))
                 nc.sync.dma_start(out=out_rows[j][:, cols], in_=res[:])
 
         for l in range(L):
             y_product(l)
-            y_turn(l)
-            v_scalar(l)
-            v_gpsimd(l)
+            y_transpose(l)
+            v_group_scalar(l, 0)
+            if l < GPSIMD_POINTS:
+                v_group_gpsimd(l)
             if l > 0:
                 y_copy_out(l - 1)
-        nc.gpsimd.tensor_tensor(out=k1[:], in0=k1_unit[:], in1=g_sb[:], op=ALU.mult)
-        quant(v_q[0], v_s[0], v_grouped[0])
-        quant(y_q[0], y_s[0], y_turned[0])
-        y_copy_out(3)
-        z_matmul(0, 0)
-        z_matmul(0, 1)
-        quant(v_q[1], v_s[1], v_grouped[1])
-        quant(y_q[1], y_s[1], y_turned[1])
-        z_matmul(1, 0)
-        z_matmul(0, 2)
-        z_matmul(0, 3)
-        nc.scalar.activation(out=k1_sign[:], in_=k1[:], func=ACT.Sign)
-        nc.scalar.activation(out=k1_safe[:], in_=k1[:], func=ACT.Copy, scale=1.0, bias=TINY)
-        h_part(0, 0, False)
-        for t in range(PACK):
-            z_first(t)
-        h_part(0, 1, False)
-        quant(v_q[2], v_s[2], v_grouped[2])
-        quant(y_q[2], y_s[2], y_turned[2])
-        z_matmul(2, 0)
-        z_matmul(1, 1)
-        quant(v_q[3], v_s[3], v_grouped[3])
-        quant(y_q[3], y_s[3], y_turned[3])
-        z_matmul(3, 0)
-        z_matmul(2, 1)
-        z_matmul(3, 1)
-        z_matmul(1, 2)
-        z_add(1, 0)
-        z_matmul(2, 2)
-        z_add(1, 1)
-        z_matmul(3, 2)
-        z_add(2, 0)
-        z_matmul(1, 3)
-        z_add(2, 1)
-        z_matmul(2, 3)
-        z_add(3, 0)
-        z_matmul(3, 3)
-        tanh_part(0)
-        z_add(3, 1)
-        clamp(0)
-        exp_part(0)
-        tanh_part(1)
-        z_add(1, 2)
-        clamp(1)
-        exp_part(1)
-        z_add(2, 2)
-        z_add(1, 3)
-        z_add(3, 2)
-        tanh_part(2)
-        z_add(2, 3)
-        clamp(2)
-        exp_part(2)
-        z_add(3, 3)
-        tanh_part(3)
-        nc.vector.reciprocal(out=inv_k1[:], in_=k1_safe[:])
-        clamp(3)
-        exp_part(3)
-        den_add(0)
-        den_add(1)
-        h_part(1, 0, True)
-        den_add(2)
-        nc.vector.scalar_tensor_tensor(out=k2_signed[:], in0=g_sb[:], scalar=3.0 * C, in1=k1_sign[:], op0=ALU.mult, op1=ALU.mult)
-        den_add(3)
-        h_part(1, 1, True)
-        quant(h_q[0], h_s[0], h_grouped[0])
-        quant(h_q[1], h_s[1], h_grouped[1])
+        give_bank("scale")
+        nc.gpsimd.tensor_tensor(out=k1[:], in0=k1_over_g[:], in1=g_sb[:], op=ALU.mult)
+        for l in range(GPSIMD_POINTS, L):
+            v_group_scalar(l, 1)
+        y_copy_out(L - 1)
 
-        inverse(0)
-        u_make(0)
-        inverse(1)
-        u_group(0, True)
-        u_make(1)
-        inverse(2)
-        u_quant_matmul(0)
-        u_make(2)
-        u_group(1, False)
-        u_quant_matmul(1)
-        inverse(3)
-        finish(0)
-        u_make(3)
-        u_group(2, False)
-        u_quant_matmul(2)
-        u_group(3, False)
-        finish(1)
-        u_quant_matmul(3)
-        finish(2)
-        finish(3)
+        chain = sorted([(step, t) for t in range(PACK) for step in range(1, L + 1)],
+                       key=lambda item: (2 * item[0] + 3 * item[1], item[1]))
+        early_tiles = range(PACK // 2)
+        waiting = [(step, t) for step, t in chain if step < L and t not in early_tiles]
+
+        def issue_waiting():
+            while waiting and free_banks:
+                z_matmul(*waiting.pop(0))
+
+        for l in range(L):
+            quantize(v_codes[l], v_scales[l], v_grouped[l])
+            if l == L - 1:
+                z_add(*chain.pop(0))
+            quantize(y_codes[l], y_scales[l], y_grouped[l])
+            for t in early_tiles:
+                z_matmul(l, t)
+            if l == 1:
+                for t in range(PACK // 2, PACK):
+                    z_matmul(0, t)
+                nc.scalar.activation(out=k1_sign[:], in_=k1[:], func=ACT.Sign)
+                nc.scalar.activation(out=k1_safe[:], in_=k1[:], func=ACT.Copy, scale=1.0, bias=TINY)
+                for h in range(2):
+                    z_first(2 * h)
+                    z_first(2 * h + 1)
+                    h_group(nc.scalar.copy, 0, h)
+        issue_waiting()
+        for step, t in chain:
+            if step < L:
+                z_add(step, t)
+                issue_waiting()
+                if step == L - 1:
+                    tanh_part(t)
+            else:
+                if t == PACK - 1:
+                    nc.vector.reciprocal(out=inv_k1[:], in_=k1_safe[:])
+                clamp_and_exp(t)
+
+        denom_sum(0)
+        denom_sum(1)
+        h_group(nc.vector.tensor_copy, 1, 0)
+        denom_sum(2)
+        nc.vector.scalar_tensor_tensor(out=k2_signed[:], in0=g_sb[:], scalar=3.0 * C, in1=k1_sign[:],
+                                       op0=ALU.mult, op1=ALU.mult)
+        denom_sum(3)
+        h_group(nc.vector.tensor_copy, 1, 1)
+        for b in range(OUT_BLOCKS):
+            quantize(h_codes[b], h_scales[b], h_grouped[b])
+
+        pieces = [(j, t) for j in range(PACK) for t in range(PACK)]
+        inverse_root(*pieces.pop(0))
+        for j in range(PACK + FINISH_LAG):
+            if j < PACK:
+                for t in range(PACK):
+                    if pieces:
+                        inverse_root(*pieces.pop(0))
+                    square(j, t)
+            if 1 <= j <= PACK:
+                u_group(j - 1)
+            if j >= FINISH_LAG:
+                finish(j - FINISH_LAG)
+            if j < PACK:
+                u_make(j)
+            if 1 <= j <= PACK:
+                u_quantize_and_matmul(j - 1)

@@ -256,29 +256,31 @@ def tile_cellfreelsfdpaminterferenceresidual_kernel(tc, y_bytes, y_scale, v, a, 
 
         chain = sorted([(step, t) for t in range(PACK) for step in range(1, L + 1)],
                        key=lambda item: (2 * item[0] + 3 * item[1], item[1]))
-        early_tiles = range(PACK // 2)
-        waiting = [(step, t) for step, t in chain if step < L and t not in early_tiles]
+        waiting = [(step, t) for step, t in chain if step < L]
+        first_of_last = waiting.index((L - 1, 0))
+        early, waiting = waiting[:first_of_last], waiting[first_of_last:]
 
         def issue_waiting():
             while waiting and free_banks:
                 z_matmul(*waiting.pop(0))
 
+        nc.scalar.activation(out=k1_sign[:], in_=k1[:], func=ACT.Sign)
+        nc.scalar.activation(out=k1_safe[:], in_=k1[:], func=ACT.Copy, scale=1.0, bias=TINY)
         for l in range(L):
             quantize(v_codes[l], v_scales[l], v_grouped[l])
             if l == L - 1:
                 z_add(*chain.pop(0))
             quantize(y_codes[l], y_scales[l], y_grouped[l])
-            for t in early_tiles:
-                z_matmul(l, t)
-            if l == 1:
-                for t in range(PACK // 2, PACK):
+            for step, t in early:
+                if step == l:
+                    z_matmul(l, t)
+            if l % 2 == 0:
+                h = l // 2
+                for t in (2 * h, 2 * h + 1):
                     z_matmul(0, t)
-                nc.scalar.activation(out=k1_sign[:], in_=k1[:], func=ACT.Sign)
-                nc.scalar.activation(out=k1_safe[:], in_=k1[:], func=ACT.Copy, scale=1.0, bias=TINY)
-                for h in range(2):
-                    z_first(2 * h)
-                    z_first(2 * h + 1)
-                    h_group(nc.scalar.copy, 0, h)
+                for t in (2 * h, 2 * h + 1):
+                    z_first(t)
+                h_group(nc.scalar.copy, 0, h)
         issue_waiting()
         for step, t in chain:
             if step < L:

import math
from contextlib import ExitStack

import concourse.mybir as mybir
from concourse.masks import make_identity

L, T, N, K, M = 4, 512, 512, 512, 1024
FLOPS = 2 * (L * T * N * K + T * K * M)

F32 = mybir.dt.float32
BF16 = mybir.dt.bfloat16
U32 = mybir.dt.uint32
U8 = mybir.dt.uint8
FP8 = mybir.dt.float8_e4m3fn
FP8X4 = mybir.dt.float8_e4m3fn_x4
ALU = mybir.AluOpType
ACT = mybir.ActivationFunctionType

P = 128
PACK = 4
BANK = 512
PSUM_BANKS = 8
HALF = 1024
OUT_BLOCKS = M // BANK
C = 1.0 / math.sqrt(5.0)
EXP_CAP = 40.0
TINY = 2.0 ** -60
GPSIMD_POINTS = 3
VECTOR_GROUPS = 2
FINISH_LAG = 3


def tile_cellfreelsfdpaminterferenceresidual_kernel(tc, y_bytes, y_scale, v, a, nv, g, h0, y0, out):
    nc = tc.nc
    with ExitStack() as ctx:
        sb = ctx.enter_context(tc.tile_pool(name="sb", bufs=1))
        ps = ctx.enter_context(tc.psum_pool(name="ps", bufs=1))
        ctx.enter_context(tc.manual_schedule())

        def sbuf(name, shape, dtype):
            return sb.tile(shape, dtype, name=name, align_bytes=64)

        def sbuf_list(name, count, shape, dtype):
            return [sbuf("%s_%d" % (name, i), shape, dtype) for i in range(count)]

        scale_col = sbuf("scale_col", [P, PACK], F32)
        nc.sync.dma_start(out=scale_col[:], in_=y_scale.rearrange("a b (p t) -> p (a b t)", t=PACK))
        nv_sb = sbuf("nv_sb", [P, PACK], BF16)
        a_sb = sbuf("a_sb", [P, L, PACK], BF16)
        g_sb = sbuf("g_sb", [P, PACK], BF16)
        nc.scalar.dma_start(out=nv_sb[:], in_=nv.rearrange("(p t) -> p t", t=PACK))
        nc.scalar.dma_start(out=a_sb[:], in_=a.rearrange("l (p t) -> p l t", t=PACK))
        nc.scalar.dma_start(out=g_sb[:], in_=g.rearrange("(p t) -> p t", t=PACK))
        y_fp8 = sbuf_list("y_fp8", L, [P, PACK * N], U8)
        v_raw = sbuf_list("v_raw", L, [P, PACK, K], BF16)
        for l in range(L):
            nc.sync.dma_start(out=y_fp8[l][:], in_=y_bytes[l].rearrange("(r j) n -> r (j n)", j=PACK))
            nc.sync.dma_start(out=v_raw[l][:], in_=v[l].rearrange("(p i) k -> p i k", i=PACK))
        h_raw = sbuf("h_raw", [P, PACK, M], BF16)
        nc.sync.dma_start(out=h_raw[:], in_=h0.rearrange("(p t) m -> p t m", t=PACK))
        y0_sb = sbuf("y0_sb", [P, PACK, M], BF16)
        nc.sync.dma_start(out=y0_sb[:], in_=y0.rearrange("(r j) m -> r j m", j=PACK))

        ident = sbuf("ident", [P, P], F32)
        make_identity(nc, ident[:])

        def channel_tile(name):
            return sbuf(name, [P, PACK], F32)

        def affine(name, src, scale, bias):
            dst = channel_tile(name)
            nc.scalar.activation(out=dst[:], in_=src[:], func=ACT.Copy, scale=scale, bias=bias)
            return dst

        inv_nv = channel_tile("inv_nv")
        nc.vector.reciprocal(out=inv_nv[:], in_=nv_sb[:])
        ratio = channel_tile("ratio")
        nc.scalar.activation(out=ratio[:], in_=inv_nv[:], func=ACT.Exp, scale=-0.8)
        log_ratio = affine("log_ratio", inv_nv, -0.8, 0.0)
        x_hi = affine("x_hi", inv_nv, 0.4, EXP_CAP / 2)
        x_lo = affine("x_lo", inv_nv, -0.4, -EXP_CAP / 2)
        one_minus_ratio = affine("one_minus_ratio", ratio, -1.0, 1.0)
        k1_over_g = affine("k1_over_g", ratio, 6.0 * C, -2.0 * C)
        c_over_nv = channel_tile("c_over_nv")
        nc.gpsimd.tensor_scalar(out=c_over_nv[:], in0=inv_nv[:], scalar1=C, scalar2=0.0, op0=ALU.mult, op1=ALU.add)
        weight = sbuf("weight", [P, L, PACK], F32)
        nc.gpsimd.tensor_tensor(out=weight[:], in0=a_sb[:],
                                in1=c_over_nv[:].unsqueeze(1).to_broadcast([P, L, PACK]), op=ALU.mult)
        k1 = channel_tile("k1")
        k1_sign = channel_tile("k1_sign")
        k1_safe = channel_tile("k1_safe")
        inv_k1 = channel_tile("inv_k1")
        k2_signed = channel_tile("k2_signed")

        free_banks = list(range(PSUM_BANKS))
        bank_of = {}
        psum = {}

        def take_bank(key, shape):
            bank_of[key] = free_banks.pop(0)
            psum[key] = ps.tile(shape, F32, name="bank_%d" % bank_of[key])
            return psum[key]

        def give_bank(key):
            free_banks.append(bank_of[key])

        scale_bank = take_bank("scale", [P, N])
        for t in range(PACK):
            nc.tensor.transpose(scale_bank[:, t:N:PACK], scale_col[:, t:t + 1].to_broadcast([P, P]), ident[:])

        y_val = {}
        y_grouped = sbuf_list("y_grouped", L, [P, T * PACK], BF16)
        v_grouped = sbuf_list("v_grouped", L, [P, K * PACK], BF16)
        y_codes = sbuf_list("y_codes", L, [P, T], U32)
        y_scales = sbuf_list("y_scales", L, [P, T], U8)
        v_codes = sbuf_list("v_codes", L, [P, K], U32)
        v_scales = sbuf_list("v_scales", L, [P, K], U8)
        x = sbuf_list("x", PACK, [P, T], F32)
        x_clamped = sbuf_list("x_clamped", PACK, [P, T], F32)
        tanh_x = sbuf_list("tanh_x", PACK, [P, T], F32)
        exp_up = sbuf_list("exp_up", PACK, [P, T], F32)
        exp_down = sbuf_list("exp_down", PACK, [P, T], F32)
        denom = sbuf_list("denom", PACK, [P, T], F32)
        h_grouped = sbuf_list("h_grouped", OUT_BLOCKS, [P, BANK * PACK], BF16)
        h_codes = sbuf_list("h_codes", OUT_BLOCKS, [P, BANK], U32)
        h_scales = sbuf_list("h_scales", OUT_BLOCKS, [P, BANK], U8)
        root = sbuf_list("root", PACK, [P, PACK * P], F32)
        frac = sbuf_list("frac", PACK, [P, PACK * P], F32)
        u_tiles = sbuf_list("u_tiles", PACK, [P, PACK * P], BF16)
        u_grouped = sbuf_list("u_grouped", PACK, [P, PACK * P], BF16)
        u_codes = sbuf_list("u_codes", PACK, [P, P], U32)
        u_scales = sbuf_list("u_scales", PACK, [P, P], U8)

        def y_product(l):
            for h in range(2):
                y_val[l, h] = sb.tile([P, 2 * N], BF16, name="y_val", bufs=4, align_bytes=64)
                for jj in range(2):
                    j = 2 * h + jj
                    nc.vector.tensor_tensor(out=y_val[l, h][:, jj * N:(jj + 1) * N],
                                            in0=y_fp8[l][:, j * N:(j + 1) * N].bitcast(FP8),
                                            in1=scale_bank[:], op=ALU.mult)

        def y_transpose(l):
            for h in range(2):
                bank = take_bank(("turn", l, h), [P, 2, 2, P])
                words = y_val[l, h][:].bitcast(F32)
                for jj in range(2):
                    for e in range(2):
                        first = jj * (N // 2) + e
                        nc.tensor.transpose(bank[:, jj, e, :], words[:, first:(jj + 1) * (N // 2):2], ident[:])

        def y_copy_out(l):
            for h in range(2):
                dst = y_grouped[l][:, h * HALF:(h + 1) * HALF].bitcast(F32)
                nc.scalar.copy(out=dst.rearrange("p (j r e) -> p j r e", j=2, e=2),
                               in_=psum["turn", l, h][:].rearrange("p j e r -> p j r e"))
                give_bank(("turn", l, h))

        def v_group_scalar(l, h):
            dst = v_grouped[l][:, h * HALF:(h + 1) * HALF].rearrange("p (t w q i) -> p w t q i", t=2, q=2, i=PACK)
            src = v_raw[l][:].rearrange("p i (w q t) -> p w t q i", q=2, t=PACK)[:, :, 2 * h:2 * h + 2]
            nc.scalar.copy(out=dst, in_=src)

        def v_group_gpsimd(l):
            dst = v_grouped[l][:, HALF:2 * HALF].rearrange("p (t q i) -> p t q i", t=2, i=PACK)
            src = v_raw[l][:].rearrange("p i (q t) -> p t q i", t=PACK)[:, 2:4]
            nc.gpsimd.tensor_scalar(out=dst, in0=src, scalar1=1.0, scalar2=0.0, op0=ALU.mult, op1=ALU.add)

        def group(copy, dst, src):
            copy(out=dst.rearrange("p (w col t) -> p w t col", col=4, t=PACK),
                 in_=src.rearrange("p t (w col) -> p w t col", col=4))

        def h_group(copy, b, h):
            first = b * BANK + h * (BANK // 2)
            group(copy, h_grouped[b][:, h * HALF:(h + 1) * HALF], h_raw[:, :, first:first + BANK // 2])

        def quantize(codes, scales, grouped):
            nc.vector.quantize_mx(out=codes[:].bitcast(FP8X4), scales=scales[:], in_=grouped[:])

        def z_matmul(l, t):
            cols = slice(t * P, (t + 1) * P)
            nc.tensor.matmul_mx(out=take_bank(("z", l, t), [P, T])[:],
                                lhsT=v_codes[l][:, cols].bitcast(FP8X4), lhsT_scale=v_scales[l][:, cols],
                                rhs=y_codes[l][:].bitcast(FP8X4), rhs_scale=y_scales[l][:], start=True, stop=True)

        def z_first(t):
            nc.scalar.activation(out=x[t][:], in_=psum["z", 0, t][:], func=ACT.Copy, scale=weight[:, 0, t:t + 1])
            give_bank(("z", 0, t))

        def z_add(l, t):
            nc.vector.scalar_tensor_tensor(out=x[t][:], in0=psum["z", l, t][:], scalar=weight[:, l, t:t + 1],
                                           in1=x[t][:], op0=ALU.mult, op1=ALU.add)
            give_bank(("z", l, t))

        def tanh_part(t):
            nc.scalar.activation(out=tanh_x[t][:], in_=x[t][:], func=ACT.Tanh, scale=k1_sign[:, t:t + 1])

        def clamp_and_exp(t):
            nc.vector.tensor_scalar(out=x_clamped[t][:], in0=x[t][:], scalar1=x_lo[:, t:t + 1],
                                    scalar2=x_hi[:, t:t + 1], op0=ALU.max, op1=ALU.min)
            for dst, scale in ((exp_up, 2.0), (exp_down, -2.0)):
                nc.scalar.activation(out=dst[t][:], in_=x_clamped[t][:], func=ACT.Exp, scale=scale,
                                     bias=log_ratio[:, t:t + 1])

        def denom_sum(t):
            nc.vector.scalar_tensor_tensor(out=denom[t][:], in0=exp_up[t][:], scalar=one_minus_ratio[:, t:t + 1],
                                           in1=exp_down[t][:], op0=ALU.add, op1=ALU.add)

        def inverse_root(j, t):
            nc.scalar.activation(out=root[j][:, t * P:(t + 1) * P], in_=denom[t][:, j * P:(j + 1) * P],
                                 func=ACT.Abs_reciprocal_sqrt, scale=inv_k1[:, t:t + 1])

        def square(j, t):
            nc.scalar.activation(out=frac[j][:, t * P:(t + 1) * P], in_=root[j][:, t * P:(t + 1) * P], func=ACT.Square)

        def u_make(j):
            for t in range(PACK):
                nc.vector.scalar_tensor_tensor(out=u_tiles[j][:, t * P:(t + 1) * P], in0=frac[j][:, t * P:(t + 1) * P],
                                               scalar=k2_signed[:, t:t + 1], in1=tanh_x[t][:, j * P:(j + 1) * P],
                                               op0=ALU.add, op1=ALU.mult)

        def u_group(j):
            copy = nc.vector.tensor_copy if j < VECTOR_GROUPS else nc.scalar.copy
            group(copy, u_grouped[j][:], u_tiles[j][:].rearrange("p (t r) -> p t r", t=PACK))

        def u_quantize_and_matmul(j):
            quantize(u_codes[j], u_scales[j], u_grouped[j])
            for b in range(OUT_BLOCKS):
                nc.tensor.matmul_mx(out=take_bank(("out", j, b), [P, BANK])[:],
                                    lhsT=u_codes[j][:].bitcast(FP8X4), lhsT_scale=u_scales[j][:],
                                    rhs=h_codes[b][:].bitcast(FP8X4), rhs_scale=h_scales[b][:], start=True, stop=True)

        out_rows = out.rearrange("(r j) m -> j r m", j=PACK)

        def finish(j):
            for b in range(OUT_BLOCKS):
                res = sb.tile([P, BANK], F32, name="res", bufs=PACK * OUT_BLOCKS, align_bytes=64)
                cols = slice(b * BANK, (b + 1) * BANK)
                nc.vector.tensor_tensor(out=res[:], in0=y0_sb[:, j, cols], in1=psum["out", j, b][:], op=ALU.subtract)
                give_bank(("out", j, b))
                nc.sync.dma_start(out=out_rows[j][:, cols], in_=res[:])

        for l in range(L):
            y_product(l)
            y_transpose(l)
            v_group_scalar(l, 0)
            if l < GPSIMD_POINTS:
                v_group_gpsimd(l)
            if l > 0:
                y_copy_out(l - 1)
        give_bank("scale")
        nc.gpsimd.tensor_tensor(out=k1[:], in0=k1_over_g[:], in1=g_sb[:], op=ALU.mult)
        for l in range(GPSIMD_POINTS, L):
            v_group_scalar(l, 1)
        y_copy_out(L - 1)

        chain = sorted([(step, t) for t in range(PACK) for step in range(1, L + 1)],
                       key=lambda item: (2 * item[0] + 3 * item[1], item[1]))
        waiting = [(step, t) for step, t in chain if step < L]
        first_of_last = waiting.index((L - 1, 0))
        early, waiting = waiting[:first_of_last], waiting[first_of_last:]

        def issue_waiting():
            while waiting and free_banks:
                z_matmul(*waiting.pop(0))

        nc.scalar.activation(out=k1_sign[:], in_=k1[:], func=ACT.Sign)
        nc.scalar.activation(out=k1_safe[:], in_=k1[:], func=ACT.Copy, scale=1.0, bias=TINY)
        for l in range(L):
            quantize(v_codes[l], v_scales[l], v_grouped[l])
            if l == L - 1:
                z_add(*chain.pop(0))
            quantize(y_codes[l], y_scales[l], y_grouped[l])
            for step, t in early:
                if step == l:
                    z_matmul(l, t)
            if l % 2 == 0:
                h = l // 2
                for t in (2 * h, 2 * h + 1):
                    z_matmul(0, t)
                for t in (2 * h, 2 * h + 1):
                    z_first(t)
                h_group(nc.scalar.copy, 0, h)
        issue_waiting()
        for step, t in chain:
            if step < L:
                z_add(step, t)
                issue_waiting()
                if step == L - 1:
                    tanh_part(t)
            else:
                if t == PACK - 1:
                    nc.vector.reciprocal(out=inv_k1[:], in_=k1_safe[:])
                clamp_and_exp(t)

        denom_sum(0)
        denom_sum(1)
        h_group(nc.vector.tensor_copy, 1, 0)
        denom_sum(2)
        nc.vector.scalar_tensor_tensor(out=k2_signed[:], in0=g_sb[:], scalar=3.0 * C, in1=k1_sign[:],
                                       op0=ALU.mult, op1=ALU.mult)
        denom_sum(3)
        h_group(nc.vector.tensor_copy, 1, 1)
        for b in range(OUT_BLOCKS):
            quantize(h_codes[b], h_scales[b], h_grouped[b])

        pieces = [(j, t) for j in range(PACK) for t in range(PACK)]
        inverse_root(*pieces.pop(0))
        for j in range(PACK + FINISH_LAG):
            if j < PACK:
                for t in range(PACK):
                    if pieces:
                        inverse_root(*pieces.pop(0))
                    square(j, t)
            if 1 <= j <= PACK:
                u_group(j - 1)
            if j >= FINISH_LAG:
                finish(j - FINISH_LAG)
            if j < PACK:
                u_make(j)
            if 1 <= j <= PACK:
                u_quantize_and_matmul(j - 1)
